import numpy as np
import ml_dtypes


def mxq(x, axis, fmt="e4m3"):
    dtype, down = {"e4m3": (ml_dtypes.float8_e4m3fn, 7), "e5m2": (ml_dtypes.float8_e5m2, 14)}[fmt]
    v = np.moveaxis(np.asarray(x, np.float32).astype(ml_dtypes.bfloat16).astype(np.float64), axis, -1)
    blocks = v.reshape(v.shape[:-1] + (-1, 32))
    amax = np.abs(blocks).max(-1, keepdims=True)
    byte = np.maximum(np.where(amax > 0, np.frexp(amax)[1] - 1 + 127, 0) - down, 1)
    scale = np.exp2(byte - 127.0)
    codes = (blocks / scale).astype(np.float32).astype(dtype).astype(np.float64)
    return np.moveaxis((codes * scale).reshape(v.shape), -1, axis)


WIDE = False


def mx_kscale(k):
    if not WIDE:
        return np.ones(k)
    levels = np.array([10, -10, 5, -5, 0])
    if k % 512:
        return np.exp2(np.random.permutation(np.resize(levels, k // 32))).repeat(32)
    a = np.empty((k // 512, 16))
    for p in range(k // 512):
        a[p, :8] = np.random.permutation(np.resize(levels, 8))
        for g in range(8):
            far = levels[np.abs(levels - a[p, g]) >= 10]
            a[p, g + 8] = far[np.random.randint(len(far))]
    return np.exp2(a.ravel()).repeat(32)


BF16 = ml_dtypes.bfloat16


def bf(x):
    return np.asarray(x, np.float32).astype(BF16)


def f64(x):
    return np.asarray(x).astype(np.float64)


B, H, C = 128, 2048, 4
HC = C * H


def draw0():
    s = mx_kscale(H)
    return {"z0": bf(np.random.standard_normal((B, H))),
            "g": bf((1.0 + 0.1 * np.random.standard_normal(H)) * s),
            "w": bf(np.random.standard_normal((H, HC)) / np.sqrt(H) / s[:, None]),
            "dx0": bf(np.random.standard_normal((B, C)) * np.sqrt(2.0 / C)),
            "dxm": bf(np.random.standard_normal((B, C)) * np.sqrt(2.0 / C))}


def vector_field(z, g, wq, channels):
    batch, hidden = z.shape
    u = z * g[None, :]
    f = np.tanh(mxq(u, 1, "e4m3") @ wq)
    return f.reshape(batch, channels, hidden)


def apply_control(f, dx):
    return np.sum(f * dx[:, :, None], axis=1)


def core(z0, g, w, dx0, dxm):
    z0, g, dx0, dxm = f64(z0), f64(g), f64(dx0), f64(dxm)
    channels = dx0.shape[1]
    wq = mxq(f64(w), 0, "e4m3")
    f0 = vector_field(z0, g, wq, channels)
    zmid = z0 + apply_control(f0, dx0)
    f1 = vector_field(zmid, g, wq, channels)
    return apply_control(f1, dxm)


def e4m3fn_bytes(y):
    return np.clip(np.asarray(y, np.float64), -448.0, 448.0).astype(np.float32).astype(ml_dtypes.float8_e4m3fn).view(np.uint8)


def e4m3fn_values(b):
    return np.asarray(b, np.uint8).view(ml_dtypes.float8_e4m3fn).astype(np.float64)


def setup_inputs():
    d = draw0()
    x0 = np.asarray(d['w']).astype(np.float64)
    s = (np.max(np.abs(x0), axis=(1,), keepdims=True) / 448.0).astype(np.float32)
    out = {}
    for k, v in d.items():
        if k == 'w':
            out['w_bytes'] = e4m3fn_bytes(x0 / s.astype(np.float64))
            out['w_scale'] = s
        else:
            out[k] = v
    return out


def reference(z0, g, w_bytes, w_scale, dx0, dxm):
    return core(z0, g, e4m3fn_values(w_bytes) * w_scale.astype(np.float64), dx0, dxm)

@@ -1,0 +1,283 @@
+from contextlib import ExitStack
+
+import concourse.mybir as mybir
+from concourse.masks import make_identity
+
+F32 = mybir.dt.float32
+BF16 = mybir.dt.bfloat16
+U32 = mybir.dt.uint32
+U8 = mybir.dt.uint8
+F8 = mybir.dt.float8_e4m3fn
+F8X4 = mybir.dt.float8_e4m3fn_x4
+ALU = mybir.AluOpType
+ACT = mybir.ActivationFunctionType
+
+P = 128
+H = 2048
+C = 4
+HC = C * H
+T = 4
+KP = P * T
+NPASS = H // KP
+BLK = 512
+NST = H // BLK
+FLOPS = 2 * 2 * P * H * HC
+NHU = 32
+
+
+def tile_neuralcdemidpointstep_w_kernel(tc, z0, g, w_bytes, w_scale, dx0, dxm, out):
+    nc = tc.nc
+    with ExitStack() as ctx:
+        pk = ctx.enter_context(tc.tile_pool(name="keep", bufs=1))
+        pr = ctx.enter_context(tc.tile_pool(name="raw", bufs=3))
+        pw = ctx.enter_context(tc.tile_pool(name="wide", bufs=3))
+        pi = ctx.enter_context(tc.tile_pool(name="inter", bufs=3))
+        ps = ctx.enter_context(tc.tile_pool(name="small", bufs=2))
+        pp = ctx.enter_context(tc.psum_pool(name="psum", bufs=1))
+        ctx.enter_context(tc.manual_schedule())
+
+        def bank(i, shape=(P, BLK)):
+            return pp.tile(list(shape), F32, name="bank%d" % i)
+
+        scl = pk.tile([P, NPASS * T], F32, name="scl")
+        z_sb = pk.tile([P, H], BF16, name="z_sb")
+        g_sb = pk.tile([P, H], BF16, name="g_sb")
+        dxb = [pk.tile([P, C], BF16, name="dxb%d" % a) for a in range(2)]
+        dxf = pk.tile([P, 2 * C], F32, name="dxf")
+        ident = pk.tile([P, P], F32, name="ident")
+        diag = pk.tile([P, C, P], F32, name="diag")
+        warm = pk.tile([P, 1], F32, name="warm")
+        codes = [[pk.tile([P, C * BLK], U32, name="codes_%d_%d" % (s, k), align_bytes=64) for k in range(NPASS)] for s in range(NST)]
+        scales = [[pk.tile([P, C * BLK], U8, name="scales_%d_%d" % (s, k), align_bytes=64) for k in range(NPASS)] for s in range(NST)]
+        zc = [[pk.tile([P, P], U32, name="zc_%d_%d" % (a, k), align_bytes=64) for k in range(NPASS)] for a in range(2)]
+        zs = [[pk.tile([P, P], U8, name="zs_%d_%d" % (a, k), align_bytes=64) for k in range(NPASS)] for a in range(2)]
+
+        nc.vector.memset(warm[:], 0.0)
+        nc.scalar.activation(out=warm[:], in_=warm[:], func=ACT.Tanh)
+
+        nc.scalar.dma_start(out=scl[:].rearrange("p (k t) -> p k t", t=T), in_=w_scale.rearrange("(k p t) o -> p k (t o)", p=P, t=T))
+
+        raws = {}
+
+        def load(i):
+            s, q, k = i // 8, (i // 4) % 2, i % 4
+            raw = pr.tile([P, T * 2 * BLK], U8, name="raw", align_bytes=64)
+            rv = raw[:].rearrange("p (t c n) -> p t c n", t=T, c=2)
+            src = w_bytes[k * KP:(k + 1) * KP, :].rearrange("(p t) m -> p t m", t=T)
+            for cc in range(2):
+                c0 = (2 * q + cc) * H + s * BLK
+                nc.sync.dma_start(out=rv[:, :, cc, :], in_=src[:, :, c0:c0 + BLK])
+            raws[i] = raw
+
+        load(0)
+        load(1)
+        nc.scalar.dma_start(out=z_sb[:], in_=z0)
+        nc.scalar.dma_start(out=g_sb[:], in_=g.partition_broadcast(P))
+        nc.scalar.dma_start(out=dxb[0][:], in_=dx0)
+        nc.scalar.dma_start(out=dxb[1][:], in_=dxm)
+        make_identity(nc, ident[:])
+
+        wides = {}
+
+        def vec_planes(i):
+            if i == 0:
+                return (2, 3)
+            return (3,) if i % 2 == 1 else ()
+
+        def widen_scalar(i):
+            k = i % 4
+            wide = pw.tile([P, T * 2 * BLK], BF16, name="wide", align_bytes=64)
+            wides[i] = wide
+            for t in range(T):
+                if t not in vec_planes(i):
+                    cols = slice(t * 2 * BLK, (t + 1) * 2 * BLK)
+                    nc.scalar.activation(out=wide[:, cols], in_=raws[i][:, cols].bitcast(F8), func=ACT.Copy, scale=scl[:, k * T + t:k * T + t + 1])
+
+        def widen_vector(i):
+            k = i % 4
+            for t in vec_planes(i):
+                cols = slice(t * 2 * BLK, (t + 1) * 2 * BLK)
+                nc.vector.tensor_scalar(out=wides[i][:, cols], in0=raws[i][:, cols].bitcast(F8), scalar1=scl[:, k * T + t:k * T + t + 1], scalar2=None, op0=ALU.mult)
+
+        inters = {}
+
+        def interleave(i, cc):
+            it = pi.tile([P, BLK * T], BF16, name="inter", align_bytes=64)
+            inters[(i, cc)] = it
+            wv = wides[i][:].rearrange("p (t c b i) -> p c b t i", t=T, c=2, i=4)[:, cc]
+            nc.vector.tensor_copy(out=it[:].rearrange("p (b i t) -> p b t i", i=4, t=T), in_=wv)
+
+        def quant(i, cc):
+            s, q, k = i // 8, (i // 4) % 2, i % 4
+            c = 2 * q + cc
+            cols = slice(c * BLK, (c + 1) * BLK)
+            nc.vector.quantize_mx(out=codes[s][k][:, cols].bitcast(F8X4), scales=scales[s][k][:, cols], in_=inters[(i, cc)][:])
+
+        def mx(acc, a, k, s, c, start, stop):
+            cols = slice(c * BLK, (c + 1) * BLK)
+            nc.tensor.matmul_mx(out=acc[:], lhsT=zc[a][k][:].bitcast(F8X4), lhsT_scale=zs[a][k][:], rhs=codes[s][k][:, cols].bitcast(F8X4), rhs_scale=scales[s][k][:, cols], start=start, stop=stop)
+
+        def turn(u, bankno):
+            xt = bank(bankno, (P, 2, P))
+            uw = u[:].bitcast(F32)
+            for h in range(2):
+                nc.tensor.transpose(xt[:, h, :], uw[:, h::2], ident[:])
+            return xt
+
+        def untangle(xt):
+            ut = ps.tile([P, P * T], BF16, name="ut", align_bytes=64)
+            nc.vector.tensor_copy(out=ut[:].bitcast(F32).rearrange("p (r u) -> p r u", u=2), in_=xt[:].rearrange("p u r -> p r u"))
+            return ut
+
+        def quant_z(a, k, ut):
+            nc.vector.quantize_mx(out=zc[a][k][:].bitcast(F8X4), scales=zs[a][k][:], in_=ut[:])
+
+        def z_head_mul(k):
+            u = ps.tile([P, BLK], BF16, name="u", align_bytes=64)
+            cols = slice(k * BLK, (k + 1) * BLK)
+            nc.vector.tensor_tensor(out=u[:], in0=z_sb[:, cols], in1=g_sb[:, cols], op=ALU.mult)
+            return u
+
+        pair_bank = {}
+        f0 = {}
+        zm = {}
+        tail = {}
+
+        def step_matmul(i):
+            s, q, k = i // 8, (i // 4) % 2, i % 4
+            pr_i = i // 4
+            for cc in range(2):
+                if k == 0:
+                    pair_bank[(pr_i, cc)] = bank(2 * (pr_i % 2) + cc)
+                mx(pair_bank[(pr_i, cc)], 0, k, s, 2 * q + cc, k == 0, k == 3)
+
+        def pair_tanh(pr_i):
+            for cc in range(2):
+                f = ps.tile([P, BLK], F32, name="f")
+                nc.scalar.activation(out=f[:], in_=pair_bank[(pr_i, cc)][:], func=ACT.Tanh)
+                f0[(pr_i, cc)] = f
+
+        def pair_diag(pr_i):
+            s, q = pr_i // 2, pr_i % 2
+            last = s == NST - 1
+            if q == 0:
+                zm[s] = bank(4)
+            for cc in range(2):
+                c = 2 * q + cc
+                nc.tensor.matmul(zm[s][:], lhsT=diag[:, c, :], rhs=f0[(pr_i, cc)][:], start=(c == 0), stop=(c == 3 or (last and c == 1)))
+
+        def z_add(s):
+            zt = ps.tile([P, BLK], F32, name="zt", bufs=1)
+            nc.vector.tensor_tensor(out=zt[:], in0=zm[s][:], in1=z_sb[:, s * BLK:(s + 1) * BLK], op=ALU.add)
+            return zt
+
+        def z_gain(s, zt):
+            u = ps.tile([P, BLK], BF16, name="u", align_bytes=64)
+            nc.vector.tensor_tensor(out=u[:], in0=zt[:], in1=g_sb[:, s * BLK:(s + 1) * BLK], op=ALU.mult)
+            return u
+
+        grp = {}
+
+        def open_groups(lst, banks):
+            for j, b in zip(lst, banks):
+                grp[j] = bank(b)
+                for k in range(NPASS - 1):
+                    mx(grp[j], 1, k, j // 4, j % 4, k == 0, False)
+
+        hold = {}
+        for n in range(NHU + 2):
+            if n + 2 < NHU:
+                load(n + 2)
+            if n < NHU:
+                widen_scalar(n)
+                widen_vector(n)
+            if n == 0:
+                nc.vector.tensor_copy(out=dxf[:, 0:C], in_=dxb[0][:])
+                nc.vector.tensor_copy(out=dxf[:, C:2 * C], in_=dxb[1][:])
+                for c in range(C):
+                    nc.vector.tensor_scalar(out=diag[:, c, :], in0=ident[:], scalar1=dxf[:, c:c + 1], scalar2=None, op0=ALU.mult)
+            m = n - 3
+            if m >= 0 and m % 4 == 3 and m != NHU - 1:
+                pair_tanh(m // 4)
+            m = n - 4
+            if m >= 0 and m % 4 == 3 and m != NHU - 1:
+                pr_i = m // 4
+                pair_diag(pr_i)
+                if pr_i == 7 - 1:
+                    hold["zt"] = z_add(3)
+            m = n - 5
+            if m >= 0 and m % 8 == 7:
+                hold["u"] = z_gain(m // 8, z_add(m // 8))
+                hold["xt"] = turn(hold["u"], 5)
+            m = n - 6
+            if m >= 0 and m % 8 == 7:
+                hold["ut"] = untangle(hold["xt"])
+            if 1 <= n <= NHU:
+                interleave(n - 1, 0)
+            if m >= 0 and m % 8 == 7:
+                quant_z(1, m // 8, hold["ut"])
+            if 2 <= n <= NHU + 1:
+                quant(n - 2, 1)
+            if 1 <= n <= NHU:
+                interleave(n - 1, 1)
+                quant(n - 1, 0)
+            if n == 1:
+                xts = []
+                for k in range(NPASS):
+                    xts.append(turn(z_head_mul(k), 4 + k))
+                hold["xts"] = xts
+            if n == 2:
+                uts = []
+                for k in range(2):
+                    uts.append(untangle(hold["xts"][k]))
+                for k in range(2):
+                    quant_z(0, k, uts[k])
+                uts = []
+                for k in range(2, 4):
+                    uts.append(untangle(hold["xts"][k]))
+                for k in range(2, 4):
+                    quant_z(0, k, uts[k - 2])
+            if n >= 2:
+                step_matmul(n - 2)
+            if n == 31:
+                open_groups((0, 1), (6, 7))
+            if n == 33:
+                open_groups((2, 3), (0, 1))
+
+        pair_tanh(7)
+        zt = hold["zt"]
+        for cc in range(2):
+            nc.vector.scalar_tensor_tensor(out=zt[:], in0=f0[(7, cc)][:], scalar=dxf[:, 2 + cc:3 + cc], in1=zt[:], op0=ALU.mult, op1=ALU.add)
+        open_groups((4, 5), (2, 3))
+        u = z_gain(3, zt)
+        xt = turn(u, 5)
+        open_groups((6,), (4,))
+        ut = untangle(xt)
+        quant_z(1, 3, ut)
+
+        accs = {}
+
+        def finish(j):
+            s, c = j // 4, j % 4
+            if c == 0:
+                accs["f"] = pw.tile([P, C * BLK], F32, name="wide", align_bytes=64)
+                accs["a"] = pi.tile([P, BLK], F32, name="inter", align_bytes=64)
+            f, a = accs["f"], accs["a"]
+            cols = slice(c * BLK, (c + 1) * BLK)
+            nc.scalar.activation(out=f[:, cols], in_=grp[j][:], func=ACT.Tanh)
+            if c == 0:
+                nc.vector.tensor_scalar(out=a[:], in0=f[:, cols], scalar1=dxf[:, C:C + 1], scalar2=None, op0=ALU.mult)
+            else:
+                nc.vector.scalar_tensor_tensor(out=a[:], in0=f[:, cols], scalar=dxf[:, C + c:C + c + 1], in1=a[:], op0=ALU.mult, op1=ALU.add)
+            if c == C - 1:
+                nc.sync.dma_start(out=out[:, s * BLK:(s + 1) * BLK], in_=a[:])
+
+        for j in range(7):
+            mx(grp[j], 1, 3, j // 4, j % 4, False, True)
+            finish(j)
+        bank_of = {0: 6, 1: 7, 2: 0, 3: 1, 4: 2, 5: 3, 6: 4, 7: 5}
+        for j in range(7, 16):
+            grp[j] = bank(bank_of[j % 8])
+            for k in range(NPASS):
+                mx(grp[j], 1, k, j // 4, j % 4, k == 0, k == 3)
+            finish(j)

@@ -23,6 +23,7 @@ BLK = 512
 NST = H // BLK
 FLOPS = 2 * 2 * P * H * HC
 NHU = 32
+VEC = [2, 2] + [1, 1, 0, 1] * 7 + [1, 2]
 
 
 def tile_neuralcdemidpointstep_w_kernel(tc, z0, g, w_bytes, w_scale, dx0, dxm, out):
@@ -31,13 +32,13 @@ def tile_neuralcdemidpointstep_w_kernel(tc, z0, g, w_bytes, w_scale, dx0, dxm, o
         pk = ctx.enter_context(tc.tile_pool(name="keep", bufs=1))
         pr = ctx.enter_context(tc.tile_pool(name="raw", bufs=3))
         pw = ctx.enter_context(tc.tile_pool(name="wide", bufs=3))
-        pi = ctx.enter_context(tc.tile_pool(name="inter", bufs=3))
+        pi = ctx.enter_context(tc.tile_pool(name="inter", bufs=2))
         ps = ctx.enter_context(tc.tile_pool(name="small", bufs=2))
         pp = ctx.enter_context(tc.psum_pool(name="psum", bufs=1))
         ctx.enter_context(tc.manual_schedule())
 
-        def bank(i, shape=(P, BLK)):
-            return pp.tile(list(shape), F32, name="bank%d" % i)
+        def bank(i, shape=(P, BLK), dt=F32):
+            return pp.tile(list(shape), dt, name="bank%d" % i)
 
         scl = pk.tile([P, NPASS * T], F32, name="scl")
         z_sb = pk.tile([P, H], BF16, name="z_sb")
@@ -45,6 +46,7 @@ def tile_neuralcdemidpointstep_w_kernel(tc, z0, g, w_bytes, w_scale, dx0, dxm, o
         dxb = [pk.tile([P, C], BF16, name="dxb%d" % a) for a in range(2)]
         dxf = pk.tile([P, 2 * C], F32, name="dxf")
         ident = pk.tile([P, P], F32, name="ident")
+        identb = pk.tile([P, P], BF16, name="identb")
         diag = pk.tile([P, C, P], F32, name="diag")
         warm = pk.tile([P, 1], F32, name="warm")
         codes = [[pk.tile([P, C * BLK], U32, name="codes_%d_%d" % (s, k), align_bytes=64) for k in range(NPASS)] for s in range(NST)]
@@ -64,25 +66,50 @@ def tile_neuralcdemidpointstep_w_kernel(tc, z0, g, w_bytes, w_scale, dx0, dxm, o
             raw = pr.tile([P, T * 2 * BLK], U8, name="raw", align_bytes=64)
             rv = raw[:].rearrange("p (t c n) -> p t c n", t=T, c=2)
             src = w_bytes[k * KP:(k + 1) * KP, :].rearrange("(p t) m -> p t m", t=T)
-            for cc in range(2):
-                c0 = (2 * q + cc) * H + s * BLK
-                nc.sync.dma_start(out=rv[:, :, cc, :], in_=src[:, :, c0:c0 + BLK])
+            if i == 0:
+                pairs = w_bytes.rearrange("(k p t) (c m) -> k p t c m", p=P, t=T, c=C)
+                for t in (0, 2, 3, 1):
+                    nc.sync.dma_start(out=rv[:, t, :, :], in_=pairs[k, :, t, 0:2, 0:BLK])
+            else:
+                for cc in range(2):
+                    c0 = (2 * q + cc) * H + s * BLK
+                    nc.sync.dma_start(out=rv[:, :, cc, :], in_=src[:, :, c0:c0 + BLK])
             raws[i] = raw
 
         load(0)
         load(1)
-        nc.scalar.dma_start(out=z_sb[:], in_=z0)
-        nc.scalar.dma_start(out=g_sb[:], in_=g.partition_broadcast(P))
-        nc.scalar.dma_start(out=dxb[0][:], in_=dx0)
-        nc.scalar.dma_start(out=dxb[1][:], in_=dxm)
         make_identity(nc, ident[:])
 
         wides = {}
 
         def vec_planes(i):
-            if i == 0:
-                return (2, 3)
-            return (3,) if i % 2 == 1 else ()
+            return tuple(range(T - VEC[i], T))
+
+        def on_pe(i, cc):
+            return i == NHU - 1 or (i % 4 == 3 and cc == 1)
+
+        zbank = {}
+
+        def pe_interleave(i, cc):
+            wv = wides[i][:].rearrange("p (t c n) -> p c n t", t=T, c=2)[:, cc]
+            for b in range(2):
+                pb = bank((6, 7, 5, 4)[2 * cc + b] if i == NHU - 1 else 6 + b, (P, 2 * BLK), BF16)
+                zbank[(i, cc, b)] = pb
+                for h in range(2):
+                    n0 = (2 * b + h) * P
+                    nc.tensor.matmul(pb[:, h * BLK:(h + 1) * BLK], lhsT=identb[:], rhs=wv[:, n0:n0 + P, :], start=True, stop=True)
+
+        def inter_tile(i):
+            if i not in inters:
+                inters[i] = pi.tile([P, 2 * BLK * T], BF16, name="inter", align_bytes=64)
+            return inters[i]
+
+        def pe_copy(i, cc, b, vec):
+            dst = inter_tile(i)[:, (2 * cc + b) * 2 * BLK:(2 * cc + b + 1) * 2 * BLK]
+            if vec:
+                nc.vector.tensor_copy(out=dst, in_=zbank[(i, cc, b)][:])
+            else:
+                nc.scalar.copy(out=dst, in_=zbank[(i, cc, b)][:])
 
         def widen_scalar(i):
             k = i % 4
@@ -101,17 +128,21 @@ def tile_neuralcdemidpointstep_w_kernel(tc, z0, g, w_bytes, w_scale, dx0, dxm, o
 
         inters = {}
 
-        def interleave(i, cc):
-            it = pi.tile([P, BLK * T], BF16, name="inter", align_bytes=64)
-            inters[(i, cc)] = it
-            wv = wides[i][:].rearrange("p (t c b i) -> p c b t i", t=T, c=2, i=4)[:, cc]
-            nc.vector.tensor_copy(out=it[:].rearrange("p (b i t) -> p b t i", i=4, t=T), in_=wv)
+        def interleave(i):
+            if on_pe(i, 0):
+                return
+            it = inter_tile(i)
+            wv = wides[i][:].rearrange("p (t m) -> p t m", t=T)
+            m = BLK if on_pe(i, 1) else 2 * BLK
+            nc.vector.tensor_copy(
+                out=it[:, 0:m * T].rearrange("p (b i t) -> p b t i", i=4, t=T),
+                in_=wv[:, :, 0:m].rearrange("p t (b i) -> p b t i", i=4))
 
         def quant(i, cc):
             s, q, k = i // 8, (i // 4) % 2, i % 4
             c = 2 * q + cc
             cols = slice(c * BLK, (c + 1) * BLK)
-            nc.vector.quantize_mx(out=codes[s][k][:, cols].bitcast(F8X4), scales=scales[s][k][:, cols], in_=inters[(i, cc)][:])
+            nc.vector.quantize_mx(out=codes[s][k][:, cols].bitcast(F8X4), scales=scales[s][k][:, cols], in_=inters[i][:, cc * BLK * T:(cc + 1) * BLK * T])
 
         def mx(acc, a, k, s, c, start, stop):
             cols = slice(c * BLK, (c + 1) * BLK)
@@ -159,12 +190,11 @@ def tile_neuralcdemidpointstep_w_kernel(tc, z0, g, w_bytes, w_scale, dx0, dxm, o
 
         def pair_diag(pr_i):
             s, q = pr_i // 2, pr_i % 2
-            last = s == NST - 1
             if q == 0:
                 zm[s] = bank(4)
             for cc in range(2):
                 c = 2 * q + cc
-                nc.tensor.matmul(zm[s][:], lhsT=diag[:, c, :], rhs=f0[(pr_i, cc)][:], start=(c == 0), stop=(c == 3 or (last and c == 1)))
+                nc.tensor.matmul(zm[s][:], lhsT=diag[:, c, :], rhs=f0[(pr_i, cc)][:], start=(c == 0), stop=(c == 3))
 
         def z_add(s):
             zt = ps.tile([P, BLK], F32, name="zt", bufs=1)
@@ -178,11 +208,11 @@ def tile_neuralcdemidpointstep_w_kernel(tc, z0, g, w_bytes, w_scale, dx0, dxm, o
 
         grp = {}
 
-        def open_groups(lst, banks):
+        def open_groups(lst, banks, close=False):
             for j, b in zip(lst, banks):
                 grp[j] = bank(b)
                 for k in range(NPASS - 1):
-                    mx(grp[j], 1, k, j // 4, j % 4, k == 0, False)
+                    mx(grp[j], 1, k, j // 4, j % 4, k == 0, close and k == NPASS - 2)
 
         hold = {}
         for n in range(NHU + 2):
@@ -190,21 +220,24 @@ def tile_neuralcdemidpointstep_w_kernel(tc, z0, g, w_bytes, w_scale, dx0, dxm, o
                 load(n + 2)
             if n < NHU:
                 widen_scalar(n)
-                widen_vector(n)
-            if n == 0:
-                nc.vector.tensor_copy(out=dxf[:, 0:C], in_=dxb[0][:])
-                nc.vector.tensor_copy(out=dxf[:, C:2 * C], in_=dxb[1][:])
-                for c in range(C):
-                    nc.vector.tensor_scalar(out=diag[:, c, :], in0=ident[:], scalar1=dxf[:, c:c + 1], scalar2=None, op0=ALU.mult)
+                if n == 0:
+                    nc.scalar.dma_start(out=z_sb[:], in_=z0)
+                    nc.scalar.dma_start(out=g_sb[:], in_=g.partition_broadcast(P))
+                    nc.scalar.dma_start(out=dxb[0][:], in_=dx0)
+                    nc.scalar.dma_start(out=dxb[1][:], in_=dxm)
+            if n >= 1:
+                for cc in range(2):
+                    if n - 1 < NHU and on_pe(n - 1, cc):
+                        pe_interleave(n - 1, cc)
+                        pe_copy(n - 1, cc, 0, False)
+                        if n - 1 < NHU - 1:
+                            pe_copy(n - 1, cc, 1, False)
             m = n - 3
             if m >= 0 and m % 4 == 3 and m != NHU - 1:
                 pair_tanh(m // 4)
             m = n - 4
-            if m >= 0 and m % 4 == 3 and m != NHU - 1:
-                pr_i = m // 4
-                pair_diag(pr_i)
-                if pr_i == 7 - 1:
-                    hold["zt"] = z_add(3)
+            if m >= 0 and m % 4 == 3 and m // 4 < 6:
+                pair_diag(m // 4)
             m = n - 5
             if m >= 0 and m % 8 == 7:
                 hold["u"] = z_gain(m // 8, z_add(m // 8))
@@ -213,20 +246,32 @@ def tile_neuralcdemidpointstep_w_kernel(tc, z0, g, w_bytes, w_scale, dx0, dxm, o
             if m >= 0 and m % 8 == 7:
                 hold["ut"] = untangle(hold["xt"])
             if 1 <= n <= NHU:
-                interleave(n - 1, 0)
-            if m >= 0 and m % 8 == 7:
-                quant_z(1, m // 8, hold["ut"])
+                if n == NHU - 1:
+                    widen_vector(n)
+                interleave(n - 1)
             if 2 <= n <= NHU + 1:
                 quant(n - 2, 1)
+            if n < NHU - 1:
+                widen_vector(n)
+            if n == NHU:
+                pe_copy(n - 1, 0, 1, True)
+            if m >= 0 and m % 8 == 7:
+                quant_z(1, m // 8, hold["ut"])
             if 1 <= n <= NHU:
-                interleave(n - 1, 1)
                 quant(n - 1, 0)
-            if n == 1:
+            if n == NHU:
+                pe_copy(n - 1, 1, 1, True)
+            if n == 3:
+                nc.vector.tensor_copy(out=identb[:], in_=ident[:])
                 xts = []
                 for k in range(NPASS):
                     xts.append(turn(z_head_mul(k), 4 + k))
                 hold["xts"] = xts
-            if n == 2:
+            if n == 4:
+                nc.vector.tensor_copy(out=dxf[:, 0:C], in_=dxb[0][:])
+                nc.vector.tensor_copy(out=dxf[:, C:2 * C], in_=dxb[1][:])
+                for c in range(C):
+                    nc.vector.tensor_scalar(out=diag[:, c, :], in0=ident[:], scalar1=dxf[:, c:c + 1], scalar2=None, op0=ALU.mult)
                 uts = []
                 for k in range(2):
                     uts.append(untangle(hold["xts"][k]))
@@ -237,21 +282,31 @@ def tile_neuralcdemidpointstep_w_kernel(tc, z0, g, w_bytes, w_scale, dx0, dxm, o
                     uts.append(untangle(hold["xts"][k]))
                 for k in range(2, 4):
                     quant_z(0, k, uts[k - 2])
-            if n >= 2:
+            if n == 5:
+                for i in range(4):
+                    step_matmul(i)
+            if n >= 6:
                 step_matmul(n - 2)
+            if n == 29:
+                open_groups((2, 5), (6, 7), True)
+            if n == 30:
+                open_groups((0, 1), (0, 1))
             if n == 31:
-                open_groups((0, 1), (6, 7))
-            if n == 33:
-                open_groups((2, 3), (0, 1))
+                zt = ps.tile([P, BLK], F32, name="zt", bufs=1)
+                nc.vector.scalar_tensor_tensor(out=zt[:], in0=f0[(6, 0)][:], scalar=dxf[:, 0:1], in1=z_sb[:, 3 * BLK:4 * BLK], op0=ALU.mult, op1=ALU.add)
+                nc.vector.scalar_tensor_tensor(out=zt[:], in0=f0[(6, 1)][:], scalar=dxf[:, 1:2], in1=zt[:], op0=ALU.mult, op1=ALU.add)
+            if n == 30:
+                spill = pr.tile([P, 2 * BLK], F32, name="raw", align_bytes=64)
+                nc.scalar.copy(out=spill[:, 0:BLK], in_=grp[2][:])
+                nc.scalar.copy(out=spill[:, BLK:2 * BLK], in_=grp[5][:])
 
         pair_tanh(7)
-        zt = hold["zt"]
         for cc in range(2):
             nc.vector.scalar_tensor_tensor(out=zt[:], in0=f0[(7, cc)][:], scalar=dxf[:, 2 + cc:3 + cc], in1=zt[:], op0=ALU.mult, op1=ALU.add)
-        open_groups((4, 5), (2, 3))
+        open_groups((3, 4, 6), (6, 7, 2))
         u = z_gain(3, zt)
         xt = turn(u, 5)
-        open_groups((6,), (4,))
+        open_groups((7, 8), (3, 4))
         ut = untangle(xt)
         quant_z(1, 3, ut)
 
@@ -261,23 +316,48 @@ def tile_neuralcdemidpointstep_w_kernel(tc, z0, g, w_bytes, w_scale, dx0, dxm, o
             s, c = j // 4, j % 4
             if c == 0:
                 accs["f"] = pw.tile([P, C * BLK], F32, name="wide", align_bytes=64)
-                accs["a"] = pi.tile([P, BLK], F32, name="inter", align_bytes=64)
-            f, a = accs["f"], accs["a"]
-            cols = slice(c * BLK, (c + 1) * BLK)
-            nc.scalar.activation(out=f[:, cols], in_=grp[j][:], func=ACT.Tanh)
-            if c == 0:
-                nc.vector.tensor_scalar(out=a[:], in0=f[:, cols], scalar1=dxf[:, C:C + 1], scalar2=None, op0=ALU.mult)
-            else:
-                nc.vector.scalar_tensor_tensor(out=a[:], in0=f[:, cols], scalar=dxf[:, C + c:C + c + 1], in1=a[:], op0=ALU.mult, op1=ALU.add)
-            if c == C - 1:
-                nc.sync.dma_start(out=out[:, s * BLK:(s + 1) * BLK], in_=a[:])
+                if j == 0:
+                    accs["a"] = pi.tile([P, C * BLK], F32, name="inter", align_bytes=64)
+            f = accs["f"]
+            a = accs["a"][:, s * BLK:(s + 1) * BLK]
+            src = spill[:, (j // 4) * BLK:(j // 4 + 1) * BLK] if j in (2, 5) else grp[j][:]
+            w = BLK // 2
+            if j < 15:
+                nc.scalar.activation(out=f[:, c * BLK:(c + 1) * BLK], in_=src, func=ACT.Tanh)
+            for h in range(2):
+                sub = slice(h * w, (h + 1) * w)
+                cols = slice(c * BLK + h * w, c * BLK + (h + 1) * w)
+                if j == 15:
+                    nc.scalar.activation(out=f[:, cols], in_=src[:, sub], func=ACT.Tanh)
+                if c == 0:
+                    nc.vector.tensor_scalar(out=a[:, sub], in0=f[:, cols], scalar1=dxf[:, C:C + 1], scalar2=None, op0=ALU.mult)
+                else:
+                    nc.vector.scalar_tensor_tensor(out=a[:, sub], in0=f[:, cols], scalar=dxf[:, C + c:C + c + 1], in1=a[:, sub], op0=ALU.mult, op1=ALU.add)
+                if j == 15:
+                    nc.sync.dma_start(out=out[:, s * BLK + h * w:s * BLK + (h + 1) * w], in_=a[:, sub])
+            if c == C - 1 and j < 15:
+                nc.sync.dma_start(out=out[:, s * BLK:(s + 1) * BLK], in_=a)
 
-        for j in range(7):
-            mx(grp[j], 1, 3, j // 4, j % 4, False, True)
-            finish(j)
-        bank_of = {0: 6, 1: 7, 2: 0, 3: 1, 4: 2, 5: 3, 6: 4, 7: 5}
-        for j in range(7, 16):
-            grp[j] = bank(bank_of[j % 8])
-            for k in range(NPASS):
-                mx(grp[j], 1, k, j // 4, j % 4, k == 0, k == 3)
-            finish(j)
+        bank_of = {2: 5, 5: 5, 9: 0, 10: 1, 11: 6, 12: 7, 13: 2, 14: 3, 15: 4}
+
+        def product(j):
+            if j in grp and j not in (2, 5):
+                mx(grp[j], 1, 3, j // 4, j % 4, False, True)
+            else:
+                grp[j] = bank(bank_of[j])
+                k0 = 3 if j in (2, 5) else 0
+                for k in range(k0, NPASS):
+                    mx(grp[j], 1, k, j // 4, j % 4, k == k0, k == 3)
+            if j in (2, 5):
+                src = spill[:, (j // 4) * BLK:(j // 4 + 1) * BLK]
+                nc.vector.tensor_tensor(out=src, in0=grp[j][:], in1=src, op=ALU.add)
+
+        order = [2, 0, 1, 3, 5, 4] + list(range(6, 16))
+        ahead = 3
+        for i in range(16):
+            if i == 0:
+                for j in order[:ahead]:
+                    product(j)
+            elif i + ahead - 1 < 16:
+                product(order[i + ahead - 1])
+            finish(i)

@@ -23,7 +23,8 @@ BLK = 512
 NST = H // BLK
 FLOPS = 2 * 2 * P * H * HC
 NHU = 32
-VEC = [2, 2] + [1, 1, 0, 1] * 7 + [1, 2]
+ZN = 4
+VEC = [2, 2] + [1, 0, 0, 1] * 7 + [0, 0]
 
 
 def tile_neuralcdemidpointstep_w_kernel(tc, z0, g, w_bytes, w_scale, dx0, dxm, out):
@@ -46,7 +47,6 @@ def tile_neuralcdemidpointstep_w_kernel(tc, z0, g, w_bytes, w_scale, dx0, dxm, o
         dxb = [pk.tile([P, C], BF16, name="dxb%d" % a) for a in range(2)]
         dxf = pk.tile([P, 2 * C], F32, name="dxf")
         ident = pk.tile([P, P], F32, name="ident")
-        identb = pk.tile([P, P], BF16, name="identb")
         diag = pk.tile([P, C, P], F32, name="diag")
         warm = pk.tile([P, 1], F32, name="warm")
         codes = [[pk.tile([P, C * BLK], U32, name="codes_%d_%d" % (s, k), align_bytes=64) for k in range(NPASS)] for s in range(NST)]
@@ -85,31 +85,10 @@ def tile_neuralcdemidpointstep_w_kernel(tc, z0, g, w_bytes, w_scale, dx0, dxm, o
         def vec_planes(i):
             return tuple(range(T - VEC[i], T))
 
-        def on_pe(i, cc):
-            return i == NHU - 1 or (i % 4 == 3 and cc == 1)
-
-        zbank = {}
-
-        def pe_interleave(i, cc):
-            wv = wides[i][:].rearrange("p (t c n) -> p c n t", t=T, c=2)[:, cc]
-            for b in range(2):
-                pb = bank((6, 7, 5, 4)[2 * cc + b] if i == NHU - 1 else 6 + b, (P, 2 * BLK), BF16)
-                zbank[(i, cc, b)] = pb
-                for h in range(2):
-                    n0 = (2 * b + h) * P
-                    nc.tensor.matmul(pb[:, h * BLK:(h + 1) * BLK], lhsT=identb[:], rhs=wv[:, n0:n0 + P, :], start=True, stop=True)
-
         def inter_tile(i):
             if i not in inters:
                 inters[i] = pi.tile([P, 2 * BLK * T], BF16, name="inter", align_bytes=64)
             return inters[i]
-
-        def pe_copy(i, cc, b, vec):
-            dst = inter_tile(i)[:, (2 * cc + b) * 2 * BLK:(2 * cc + b + 1) * 2 * BLK]
-            if vec:
-                nc.vector.tensor_copy(out=dst, in_=zbank[(i, cc, b)][:])
-            else:
-                nc.scalar.copy(out=dst, in_=zbank[(i, cc, b)][:])
 
         def widen_scalar(i):
             k = i % 4
@@ -128,15 +107,11 @@ def tile_neuralcdemidpointstep_w_kernel(tc, z0, g, w_bytes, w_scale, dx0, dxm, o
 
         inters = {}
 
-        def interleave(i):
-            if on_pe(i, 0):
-                return
-            it = inter_tile(i)
+        def interleave(copy, i, m0, m1):
             wv = wides[i][:].rearrange("p (t m) -> p t m", t=T)
-            m = BLK if on_pe(i, 1) else 2 * BLK
-            nc.vector.tensor_copy(
-                out=it[:, 0:m * T].rearrange("p (b i t) -> p b t i", i=4, t=T),
-                in_=wv[:, :, 0:m].rearrange("p t (b i) -> p b t i", i=4))
+            copy(
+                out=inter_tile(i)[:, m0 * T:m1 * T].rearrange("p (b i t) -> p b t i", i=4, t=T),
+                in_=wv[:, :, m0:m1].rearrange("p t (b i) -> p b t i", i=4))
 
         def quant(i, cc):
             s, q, k = i // 8, (i // 4) % 2, i % 4
@@ -218,56 +193,49 @@ def tile_neuralcdemidpointstep_w_kernel(tc, z0, g, w_bytes, w_scale, dx0, dxm, o
         for n in range(NHU + 2):
             if n + 2 < NHU:
                 load(n + 2)
+            if n == 0:
+                nc.sync.dma_start(out=z_sb[:], in_=z0)
+            if n in (1, 2):
+                nc.sync.dma_start(out=g_sb[:, (n - 1) * H // 2:n * H // 2], in_=g[(n - 1) * H // 2:n * H // 2].partition_broadcast(P))
+            if n == 3:
+                nc.sync.dma_start(out=dxb[0][:], in_=dx0)
+                nc.sync.dma_start(out=dxb[1][:], in_=dxm)
             if n < NHU:
                 widen_scalar(n)
-                if n == 0:
-                    nc.scalar.dma_start(out=z_sb[:], in_=z0)
-                    nc.scalar.dma_start(out=g_sb[:], in_=g.partition_broadcast(P))
-                    nc.scalar.dma_start(out=dxb[0][:], in_=dx0)
-                    nc.scalar.dma_start(out=dxb[1][:], in_=dxm)
-            if n >= 1:
-                for cc in range(2):
-                    if n - 1 < NHU and on_pe(n - 1, cc):
-                        pe_interleave(n - 1, cc)
-                        pe_copy(n - 1, cc, 0, False)
-                        if n - 1 < NHU - 1:
-                            pe_copy(n - 1, cc, 1, False)
-            m = n - 3
+            if n == NHU:
+                interleave(nc.scalar.copy, n - 1, 3 * BLK // 2, 2 * BLK)
+            m = n - (4 if n < 8 else 3)
             if m >= 0 and m % 4 == 3 and m != NHU - 1:
                 pair_tanh(m // 4)
-            m = n - 4
+            m = n - (5 if n < 9 else 4)
             if m >= 0 and m % 4 == 3 and m // 4 < 6:
                 pair_diag(m // 4)
-            m = n - 5
-            if m >= 0 and m % 8 == 7:
-                hold["u"] = z_gain(m // 8, z_add(m // 8))
-                hold["xt"] = turn(hold["u"], 5)
+            mg = n - 5
+            if mg >= 0 and mg % 8 == 7:
+                hold["zt"] = z_add(mg // 8)
             m = n - 6
             if m >= 0 and m % 8 == 7:
                 hold["ut"] = untangle(hold["xt"])
             if 1 <= n <= NHU:
-                if n == NHU - 1:
-                    widen_vector(n)
-                interleave(n - 1)
+                interleave(nc.vector.tensor_copy, n - 1, 0, BLK if n == NHU else 2 * BLK)
             if 2 <= n <= NHU + 1:
                 quant(n - 2, 1)
-            if n < NHU - 1:
+            if mg >= 0 and mg % 8 == 7:
+                hold["xt"] = turn(z_gain(mg // 8, hold["zt"]), 5)
+            if n < NHU:
                 widen_vector(n)
             if n == NHU:
-                pe_copy(n - 1, 0, 1, True)
+                interleave(nc.vector.tensor_copy, n - 1, BLK, 3 * BLK // 2)
             if m >= 0 and m % 8 == 7:
                 quant_z(1, m // 8, hold["ut"])
             if 1 <= n <= NHU:
                 quant(n - 1, 0)
-            if n == NHU:
-                pe_copy(n - 1, 1, 1, True)
-            if n == 3:
-                nc.vector.tensor_copy(out=identb[:], in_=ident[:])
+            if n == ZN:
                 xts = []
                 for k in range(NPASS):
                     xts.append(turn(z_head_mul(k), 4 + k))
                 hold["xts"] = xts
-            if n == 4:
+            if n == ZN + 1:
                 nc.vector.tensor_copy(out=dxf[:, 0:C], in_=dxb[0][:])
                 nc.vector.tensor_copy(out=dxf[:, C:2 * C], in_=dxb[1][:])
                 for c in range(C):
@@ -282,10 +250,10 @@ def tile_neuralcdemidpointstep_w_kernel(tc, z0, g, w_bytes, w_scale, dx0, dxm, o
                     uts.append(untangle(hold["xts"][k]))
                 for k in range(2, 4):
                     quant_z(0, k, uts[k - 2])
-            if n == 5:
-                for i in range(4):
+            if n == ZN + 2:
+                for i in range(ZN + 1):
                     step_matmul(i)
-            if n >= 6:
+            if n > ZN + 2:
                 step_matmul(n - 2)
             if n == 29:
                 open_groups((2, 5), (6, 7), True)
@@ -300,11 +268,17 @@ def tile_neuralcdemidpointstep_w_kernel(tc, z0, g, w_bytes, w_scale, dx0, dxm, o
                 nc.scalar.copy(out=spill[:, 0:BLK], in_=grp[2][:])
                 nc.scalar.copy(out=spill[:, BLK:2 * BLK], in_=grp[5][:])
 
-        pair_tanh(7)
+        u = ps.tile([P, BLK], BF16, name="u", align_bytes=64)
+        halves = [slice(0, BLK // 2), slice(BLK // 2, BLK)]
         for cc in range(2):
-            nc.vector.scalar_tensor_tensor(out=zt[:], in0=f0[(7, cc)][:], scalar=dxf[:, 2 + cc:3 + cc], in1=zt[:], op0=ALU.mult, op1=ALU.add)
+            f = ps.tile([P, BLK], F32, name="f")
+            for sub in halves if cc else [slice(0, BLK)]:
+                nc.scalar.activation(out=f[:, sub], in_=pair_bank[(7, cc)][:, sub], func=ACT.Tanh)
+            for sub in halves:
+                nc.vector.scalar_tensor_tensor(out=zt[:, sub], in0=f[:, sub], scalar=dxf[:, 2 + cc:3 + cc], in1=zt[:, sub], op0=ALU.mult, op1=ALU.add)
+        for sub in halves:
+            nc.vector.tensor_tensor(out=u[:, sub], in0=zt[:, sub], in1=g_sb[:, 3 * BLK + sub.start:3 * BLK + sub.stop], op=ALU.mult)
         open_groups((3, 4, 6), (6, 7, 2))
-        u = z_gain(3, zt)
         xt = turn(u, 5)
         open_groups((7, 8), (3, 4))
         ut = untangle(xt)

from contextlib import ExitStack

import concourse.mybir as mybir
from concourse.masks import make_identity

F32 = mybir.dt.float32
BF16 = mybir.dt.bfloat16
U32 = mybir.dt.uint32
U8 = mybir.dt.uint8
F8 = mybir.dt.float8_e4m3fn
F8X4 = mybir.dt.float8_e4m3fn_x4
ALU = mybir.AluOpType
ACT = mybir.ActivationFunctionType

P = 128
H = 2048
C = 4
HC = C * H
T = 4
KP = P * T
NPASS = H // KP
BLK = 512
NST = H // BLK
FLOPS = 2 * 2 * P * H * HC
NHU = 32
ZN = 4
VEC = [2, 2] + [1, 0, 0, 1] * 7 + [0, 0]


def tile_neuralcdemidpointstep_w_kernel(tc, z0, g, w_bytes, w_scale, dx0, dxm, out):
    nc = tc.nc
    with ExitStack() as ctx:
        pk = ctx.enter_context(tc.tile_pool(name="keep", bufs=1))
        pr = ctx.enter_context(tc.tile_pool(name="raw", bufs=3))
        pw = ctx.enter_context(tc.tile_pool(name="wide", bufs=3))
        pi = ctx.enter_context(tc.tile_pool(name="inter", bufs=2))
        ps = ctx.enter_context(tc.tile_pool(name="small", bufs=2))
        pp = ctx.enter_context(tc.psum_pool(name="psum", bufs=1))
        ctx.enter_context(tc.manual_schedule())

        def bank(i, shape=(P, BLK), dt=F32):
            return pp.tile(list(shape), dt, name="bank%d" % i)

        scl = pk.tile([P, NPASS * T], F32, name="scl")
        z_sb = pk.tile([P, H], BF16, name="z_sb")
        g_sb = pk.tile([P, H], BF16, name="g_sb")
        dxb = [pk.tile([P, C], BF16, name="dxb%d" % a) for a in range(2)]
        dxf = pk.tile([P, 2 * C], F32, name="dxf")
        ident = pk.tile([P, P], F32, name="ident")
        diag = pk.tile([P, C, P], F32, name="diag")
        warm = pk.tile([P, 1], F32, name="warm")
        codes = [[pk.tile([P, C * BLK], U32, name="codes_%d_%d" % (s, k), align_bytes=64) for k in range(NPASS)] for s in range(NST)]
        scales = [[pk.tile([P, C * BLK], U8, name="scales_%d_%d" % (s, k), align_bytes=64) for k in range(NPASS)] for s in range(NST)]
        zc = [[pk.tile([P, P], U32, name="zc_%d_%d" % (a, k), align_bytes=64) for k in range(NPASS)] for a in range(2)]
        zs = [[pk.tile([P, P], U8, name="zs_%d_%d" % (a, k), align_bytes=64) for k in range(NPASS)] for a in range(2)]

        nc.vector.memset(warm[:], 0.0)
        nc.scalar.activation(out=warm[:], in_=warm[:], func=ACT.Tanh)

        nc.scalar.dma_start(out=scl[:].rearrange("p (k t) -> p k t", t=T), in_=w_scale.rearrange("(k p t) o -> p k (t o)", p=P, t=T))

        raws = {}

        def load(i):
            s, q, k = i // 8, (i // 4) % 2, i % 4
            raw = pr.tile([P, T * 2 * BLK], U8, name="raw", align_bytes=64)
            rv = raw[:].rearrange("p (t c n) -> p t c n", t=T, c=2)
            src = w_bytes[k * KP:(k + 1) * KP, :].rearrange("(p t) m -> p t m", t=T)
            if i == 0:
                pairs = w_bytes.rearrange("(k p t) (c m) -> k p t c m", p=P, t=T, c=C)
                for t in (0, 2, 3, 1):
                    nc.sync.dma_start(out=rv[:, t, :, :], in_=pairs[k, :, t, 0:2, 0:BLK])
            else:
                for cc in range(2):
                    c0 = (2 * q + cc) * H + s * BLK
                    nc.sync.dma_start(out=rv[:, :, cc, :], in_=src[:, :, c0:c0 + BLK])
            raws[i] = raw

        load(0)
        load(1)
        make_identity(nc, ident[:])

        wides = {}

        def vec_planes(i):
            return tuple(range(T - VEC[i], T))

        def inter_tile(i):
            if i not in inters:
                inters[i] = pi.tile([P, 2 * BLK * T], BF16, name="inter", align_bytes=64)
            return inters[i]

        def widen_scalar(i):
            k = i % 4
            wide = pw.tile([P, T * 2 * BLK], BF16, name="wide", align_bytes=64)
            wides[i] = wide
            for t in range(T):
                if t not in vec_planes(i):
                    cols = slice(t * 2 * BLK, (t + 1) * 2 * BLK)
                    nc.scalar.activation(out=wide[:, cols], in_=raws[i][:, cols].bitcast(F8), func=ACT.Copy, scale=scl[:, k * T + t:k * T + t + 1])

        def widen_vector(i):
            k = i % 4
            for t in vec_planes(i):
                cols = slice(t * 2 * BLK, (t + 1) * 2 * BLK)
                nc.vector.tensor_scalar(out=wides[i][:, cols], in0=raws[i][:, cols].bitcast(F8), scalar1=scl[:, k * T + t:k * T + t + 1], scalar2=None, op0=ALU.mult)

        inters = {}

        def interleave(copy, i, m0, m1):
            wv = wides[i][:].rearrange("p (t m) -> p t m", t=T)
            copy(
                out=inter_tile(i)[:, m0 * T:m1 * T].rearrange("p (b i t) -> p b t i", i=4, t=T),
                in_=wv[:, :, m0:m1].rearrange("p t (b i) -> p b t i", i=4))

        def quant(i, cc):
            s, q, k = i // 8, (i // 4) % 2, i % 4
            c = 2 * q + cc
            cols = slice(c * BLK, (c + 1) * BLK)
            nc.vector.quantize_mx(out=codes[s][k][:, cols].bitcast(F8X4), scales=scales[s][k][:, cols], in_=inters[i][:, cc * BLK * T:(cc + 1) * BLK * T])

        def mx(acc, a, k, s, c, start, stop):
            cols = slice(c * BLK, (c + 1) * BLK)
            nc.tensor.matmul_mx(out=acc[:], lhsT=zc[a][k][:].bitcast(F8X4), lhsT_scale=zs[a][k][:], rhs=codes[s][k][:, cols].bitcast(F8X4), rhs_scale=scales[s][k][:, cols], start=start, stop=stop)

        def turn(u, bankno):
            xt = bank(bankno, (P, 2, P))
            uw = u[:].bitcast(F32)
            for h in range(2):
                nc.tensor.transpose(xt[:, h, :], uw[:, h::2], ident[:])
            return xt

        def untangle(xt):
            ut = ps.tile([P, P * T], BF16, name="ut", align_bytes=64)
            nc.vector.tensor_copy(out=ut[:].bitcast(F32).rearrange("p (r u) -> p r u", u=2), in_=xt[:].rearrange("p u r -> p r u"))
            return ut

        def quant_z(a, k, ut):
            nc.vector.quantize_mx(out=zc[a][k][:].bitcast(F8X4), scales=zs[a][k][:], in_=ut[:])

        def z_head_mul(k):
            u = ps.tile([P, BLK], BF16, name="u", align_bytes=64)
            cols = slice(k * BLK, (k + 1) * BLK)
            nc.vector.tensor_tensor(out=u[:], in0=z_sb[:, cols], in1=g_sb[:, cols], op=ALU.mult)
            return u

        pair_bank = {}
        f0 = {}
        zm = {}
        tail = {}

        def step_matmul(i):
            s, q, k = i // 8, (i // 4) % 2, i % 4
            pr_i = i // 4
            for cc in range(2):
                if k == 0:
                    pair_bank[(pr_i, cc)] = bank(2 * (pr_i % 2) + cc)
                mx(pair_bank[(pr_i, cc)], 0, k, s, 2 * q + cc, k == 0, k == 3)

        def pair_tanh(pr_i):
            for cc in range(2):
                f = ps.tile([P, BLK], F32, name="f")
                nc.scalar.activation(out=f[:], in_=pair_bank[(pr_i, cc)][:], func=ACT.Tanh)
                f0[(pr_i, cc)] = f

        def pair_diag(pr_i):
            s, q = pr_i // 2, pr_i % 2
            if q == 0:
                zm[s] = bank(4)
            for cc in range(2):
                c = 2 * q + cc
                nc.tensor.matmul(zm[s][:], lhsT=diag[:, c, :], rhs=f0[(pr_i, cc)][:], start=(c == 0), stop=(c == 3))

        def z_add(s):
            zt = ps.tile([P, BLK], F32, name="zt", bufs=1)
            nc.vector.tensor_tensor(out=zt[:], in0=zm[s][:], in1=z_sb[:, s * BLK:(s + 1) * BLK], op=ALU.add)
            return zt

        def z_gain(s, zt):
            u = ps.tile([P, BLK], BF16, name="u", align_bytes=64)
            nc.vector.tensor_tensor(out=u[:], in0=zt[:], in1=g_sb[:, s * BLK:(s + 1) * BLK], op=ALU.mult)
            return u

        grp = {}

        def open_groups(lst, banks, close=False):
            for j, b in zip(lst, banks):
                grp[j] = bank(b)
                for k in range(NPASS - 1):
                    mx(grp[j], 1, k, j // 4, j % 4, k == 0, close and k == NPASS - 2)

        hold = {}
        for n in range(NHU + 2):
            if n + 2 < NHU:
                load(n + 2)
            if n == 0:
                nc.sync.dma_start(out=z_sb[:], in_=z0)
            if n in (1, 2):
                nc.sync.dma_start(out=g_sb[:, (n - 1) * H // 2:n * H // 2], in_=g[(n - 1) * H // 2:n * H // 2].partition_broadcast(P))
            if n == 3:
                nc.sync.dma_start(out=dxb[0][:], in_=dx0)
                nc.sync.dma_start(out=dxb[1][:], in_=dxm)
            if n < NHU:
                widen_scalar(n)
            if n == NHU:
                interleave(nc.scalar.copy, n - 1, 3 * BLK // 2, 2 * BLK)
            m = n - (4 if n < 8 else 3)
            if m >= 0 and m % 4 == 3 and m != NHU - 1:
                pair_tanh(m // 4)
            m = n - (5 if n < 9 else 4)
            if m >= 0 and m % 4 == 3 and m // 4 < 6:
                pair_diag(m // 4)
            mg = n - 5
            if mg >= 0 and mg % 8 == 7:
                hold["zt"] = z_add(mg // 8)
            m = n - 6
            if m >= 0 and m % 8 == 7:
                hold["ut"] = untangle(hold["xt"])
            if 1 <= n <= NHU:
                interleave(nc.vector.tensor_copy, n - 1, 0, BLK if n == NHU else 2 * BLK)
            if 2 <= n <= NHU + 1:
                quant(n - 2, 1)
            if mg >= 0 and mg % 8 == 7:
                hold["xt"] = turn(z_gain(mg // 8, hold["zt"]), 5)
            if n < NHU:
                widen_vector(n)
            if n == NHU:
                interleave(nc.vector.tensor_copy, n - 1, BLK, 3 * BLK // 2)
            if m >= 0 and m % 8 == 7:
                quant_z(1, m // 8, hold["ut"])
            if 1 <= n <= NHU:
                quant(n - 1, 0)
            if n == ZN:
                xts = []
                for k in range(NPASS):
                    xts.append(turn(z_head_mul(k), 4 + k))
                hold["xts"] = xts
            if n == ZN + 1:
                nc.vector.tensor_copy(out=dxf[:, 0:C], in_=dxb[0][:])
                nc.vector.tensor_copy(out=dxf[:, C:2 * C], in_=dxb[1][:])
                for c in range(C):
                    nc.vector.tensor_scalar(out=diag[:, c, :], in0=ident[:], scalar1=dxf[:, c:c + 1], scalar2=None, op0=ALU.mult)
                uts = []
                for k in range(2):
                    uts.append(untangle(hold["xts"][k]))
                for k in range(2):
                    quant_z(0, k, uts[k])
                uts = []
                for k in range(2, 4):
                    uts.append(untangle(hold["xts"][k]))
                for k in range(2, 4):
                    quant_z(0, k, uts[k - 2])
            if n == ZN + 2:
                for i in range(ZN + 1):
                    step_matmul(i)
            if n > ZN + 2:
                step_matmul(n - 2)
            if n == 29:
                open_groups((2, 5), (6, 7), True)
            if n == 30:
                open_groups((0, 1), (0, 1))
            if n == 31:
                zt = ps.tile([P, BLK], F32, name="zt", bufs=1)
                nc.vector.scalar_tensor_tensor(out=zt[:], in0=f0[(6, 0)][:], scalar=dxf[:, 0:1], in1=z_sb[:, 3 * BLK:4 * BLK], op0=ALU.mult, op1=ALU.add)
                nc.vector.scalar_tensor_tensor(out=zt[:], in0=f0[(6, 1)][:], scalar=dxf[:, 1:2], in1=zt[:], op0=ALU.mult, op1=ALU.add)
            if n == 30:
                spill = pr.tile([P, 2 * BLK], F32, name="raw", align_bytes=64)
                nc.scalar.copy(out=spill[:, 0:BLK], in_=grp[2][:])
                nc.scalar.copy(out=spill[:, BLK:2 * BLK], in_=grp[5][:])

        u = ps.tile([P, BLK], BF16, name="u", align_bytes=64)
        halves = [slice(0, BLK // 2), slice(BLK // 2, BLK)]
        for cc in range(2):
            f = ps.tile([P, BLK], F32, name="f")
            for sub in halves if cc else [slice(0, BLK)]:
                nc.scalar.activation(out=f[:, sub], in_=pair_bank[(7, cc)][:, sub], func=ACT.Tanh)
            for sub in halves:
                nc.vector.scalar_tensor_tensor(out=zt[:, sub], in0=f[:, sub], scalar=dxf[:, 2 + cc:3 + cc], in1=zt[:, sub], op0=ALU.mult, op1=ALU.add)
        for sub in halves:
            nc.vector.tensor_tensor(out=u[:, sub], in0=zt[:, sub], in1=g_sb[:, 3 * BLK + sub.start:3 * BLK + sub.stop], op=ALU.mult)
        open_groups((3, 4, 6), (6, 7, 2))
        xt = turn(u, 5)
        open_groups((7, 8), (3, 4))
        ut = untangle(xt)
        quant_z(1, 3, ut)

        accs = {}

        def finish(j):
            s, c = j // 4, j % 4
            if c == 0:
                accs["f"] = pw.tile([P, C * BLK], F32, name="wide", align_bytes=64)
                if j == 0:
                    accs["a"] = pi.tile([P, C * BLK], F32, name="inter", align_bytes=64)
            f = accs["f"]
            a = accs["a"][:, s * BLK:(s + 1) * BLK]
            src = spill[:, (j // 4) * BLK:(j // 4 + 1) * BLK] if j in (2, 5) else grp[j][:]
            w = BLK // 2
            if j < 15:
                nc.scalar.activation(out=f[:, c * BLK:(c + 1) * BLK], in_=src, func=ACT.Tanh)
            for h in range(2):
                sub = slice(h * w, (h + 1) * w)
                cols = slice(c * BLK + h * w, c * BLK + (h + 1) * w)
                if j == 15:
                    nc.scalar.activation(out=f[:, cols], in_=src[:, sub], func=ACT.Tanh)
                if c == 0:
                    nc.vector.tensor_scalar(out=a[:, sub], in0=f[:, cols], scalar1=dxf[:, C:C + 1], scalar2=None, op0=ALU.mult)
                else:
                    nc.vector.scalar_tensor_tensor(out=a[:, sub], in0=f[:, cols], scalar=dxf[:, C + c:C + c + 1], in1=a[:, sub], op0=ALU.mult, op1=ALU.add)
                if j == 15:
                    nc.sync.dma_start(out=out[:, s * BLK + h * w:s * BLK + (h + 1) * w], in_=a[:, sub])
            if c == C - 1 and j < 15:
                nc.sync.dma_start(out=out[:, s * BLK:(s + 1) * BLK], in_=a)

        bank_of = {2: 5, 5: 5, 9: 0, 10: 1, 11: 6, 12: 7, 13: 2, 14: 3, 15: 4}

        def product(j):
            if j in grp and j not in (2, 5):
                mx(grp[j], 1, 3, j // 4, j % 4, False, True)
            else:
                grp[j] = bank(bank_of[j])
                k0 = 3 if j in (2, 5) else 0
                for k in range(k0, NPASS):
                    mx(grp[j], 1, k, j // 4, j % 4, k == k0, k == 3)
            if j in (2, 5):
                src = spill[:, (j // 4) * BLK:(j // 4 + 1) * BLK]
                nc.vector.tensor_tensor(out=src, in0=grp[j][:], in1=src, op=ALU.add)

        order = [2, 0, 1, 3, 5, 4] + list(range(6, 16))
        ahead = 3
        for i in range(16):
            if i == 0:
                for j in order[:ahead]:
                    product(j)
            elif i + ahead - 1 < 16:
                product(order[i + ahead - 1])
            finish(i)
